import numpy as np, ml_dtypes
CORES = [3,11,19,27,35,43]
N = 6
import mx_ref
BF = ml_dtypes.bfloat16
def entries(a):
    return np.ascontiguousarray(a.T).reshape(-1)
def table(e):
    return np.ascontiguousarray(np.reshape(e, (-1, 16)).T).astype(np.int32)
def f(rng, *shape):
    return mx_ref.flush((rng.standard_normal(shape, dtype=np.float32) * np.exp2(rng.integers(-2, 3, shape[:-1] + (1,)))).astype(BF))
def wide(rng, *shape, cols=0):
    v = rng.standard_normal(shape, dtype=np.float32) * np.exp2(rng.integers(-12, 13, shape)).astype(np.float32)
    if cols: v *= np.repeat(np.exp2(rng.integers(-cols, cols + 1, shape[:-2] + (1, shape[-1] // 4))) * (rng.random(shape[:-2] + (1, shape[-1] // 4)) > 0.0625), 4, axis=-1).astype(np.float32)
    return mx_ref.flush(v.astype(BF))
T, ND, CD, LM, CAPP = 768, 64, 16, 64, 160
def lens(rng, n, total):
    a = 1 + np.minimum(LM - 1, rng.multinomial(total - n, rng.dirichlet(np.ones(n))))
    for i in rng.permutation(n): a[i] += min(LM - a[i], total - a.sum())
    return a
def places(rng, l):
    o = rng.permutation(ND); g = rng.multinomial(T - l.sum(), rng.dirichlet(np.ones(ND + 1)))
    s = np.zeros(ND, int); s[o] = np.cumsum(g[:ND]) + np.cumsum(l[o]) - l[o]
    return s
def pick(rng, l):
    p = rng.permutation(ND); a, b = p[:CD].copy(), p[CD:].copy()
    while l[a].sum() > CAPP:
        i = np.argmax(l[a]); j = rng.choice(np.flatnonzero(l[b] < l[a[i]]))
        a[i], b[j] = b[j], a[i]
    return rng.permutation(a)
def lists(rng, kind="any"):
    s, n, c = [], [], np.zeros((N, N * CD), int)
    K, J = (T - ND) // (LM - 1), (CAPP - CD) // (LM - 1)
    TT = min(T, ND // CD * CAPP)
    for q in range(N):
        d = rng.permutation(ND); l = np.ones(ND, int)
        if kind == "long": l[d[:K]] = LM
        elif kind == "full": l[d] = np.concatenate([lens(rng, CD, CAPP), lens(rng, CD, CAPP), lens(rng, ND - 2 * CD, T - 2 * CAPP)])
        elif kind == "any": l[d] = lens(rng, ND, int(rng.integers(TT - TT // 4, TT + 1)))
        s.append(table(places(rng, l))); n.append(table(l))
        for r in range(N):
            if kind == "long": e = rng.permutation(np.concatenate([rng.permutation(d[:K])[:J], rng.permutation(d[K:])[:CD - J]]))
            elif kind == "full": k = CD * int(rng.integers(0, 2)); e = rng.permutation(d[k:k + CD])
            else: e = pick(rng, l)
            c[r, CD * q:CD * q + CD] = e
    return {"st": np.stack(s), "ln": np.stack(n), "cd": np.stack([table(c[r]) for r in range(N)])}
def setup_inputs(rng):
    return {"x": f(rng, N, 128, 4 * T), "qw": f(rng, N, 128, 512), **lists(rng)}
def setup_inputs_long(rng):
    return {**setup_inputs(rng), **lists(rng, "long")}
def setup_inputs_ones(rng):
    return {**setup_inputs(rng), **lists(rng, "ones")}
def setup_inputs_full(rng):
    return {**setup_inputs(rng), **lists(rng, "full")}
def setup_inputs_below(rng):
    d = setup_inputs(rng); p = rng.permutation(N)
    s, u = rng.integers(-20, 27, N), rng.integers(-20, 28, N)
    s[p[0]] = 26; u[rng.choice(p[:-1])] = 27; s[p[-1]] = 0; u[p[-1]] = 0
    d["x"] = mx_ref.flush((-np.exp2(rng.uniform(-3, 3, (N, 128, 4 * T)) + s[:, None, None])).astype(BF))
    d["qw"] = mx_ref.flush(np.exp2(rng.uniform(-2, 2, (N, 128, 512)) + u[:, None, None]).astype(BF))
    return d
def setup_inputs_spread(rng):
    d = setup_inputs(rng); d["x"] = wide(rng, N, 128, 4 * T, cols=8); return d
def check_inputs(d):
    b = []
    L = [entries(d["ln"][r]).astype(np.int64) for r in range(N)]
    for r in range(N):
        s, l = entries(d["st"][r]).astype(np.int64), L[r]
        if l.min() < 1 or l.max() > LM: b.append("ln")
        o = np.argsort(s, kind="stable")
        if s.min() < 0 or (s + l).max() > T or (s[o][:-1] + l[o][:-1] > s[o][1:]).any(): b.append("st")
        c = entries(d["cd"][r])
        if c.min() < 0 or c.max() >= ND: b.append("cd"); continue
        for q in range(N):
            e = c[CD * q:CD * q + CD]
            if len(set(e.tolist())) != CD or L[q][e].sum() > CAPP: b.append("cd")
    return sorted(set(b))
def reference(x, qw, st, ln, cd):
    X = [mx_ref.quantize(x[q]) for q in range(N)]
    y = np.zeros((N, 128, N * CD), np.float32)
    for r in range(N):
        W = mx_ref.quantize(qw[r]); c = entries(cd[r])
        for q in range(N):
            z = mx_ref.matmul(W, X[q]); s, l = entries(st[q]), entries(ln[q])
            for i in range(CD * q, CD * q + CD):
                y[r][:, i] = z[:, s[c[i]]:s[c[i]] + l[c[i]]].max(axis=1)
    return {"y": y}

@@ -1,0 +1,311 @@
+import numpy as np
+from concourse.bass import DstId, RemoteDMATransfer
+from concourse.mybir import dt, AluOpType, ActivationFunctionType
+
+N, CD, ND, TOK, CAP = 6, 16, 64, 768, 160
+S = N - 1
+VW = CAP + 8
+XW = 4 * (TOK + CAP)
+HI = 4096
+MW = N * CAP + 8
+BIG = 1.0e29
+
+SCRATCH = {
+    "cdi": ("sbuf", [128, N], "int32"),
+    "cdu": ("sbuf", [128, N], "uint16"),
+    "cdl": ("sbuf", [128, N * S], "uint16"),
+    "cdx": ("sbuf", [128, 8], "uint16"),
+    "cdown": ("sbuf", [128, 2], "uint16"),
+    "raw": ("sbuf", [128, 2 * ND], "int32"),
+    "bc": ("sbuf", [128, 2 * ND], "int32"),
+    "tabs": ("sbuf", [128, ND], "float32"),
+    "tabl": ("sbuf", [128, ND], "float32"),
+    "ip": ("sbuf", [128, 1], "int32"),
+    "ii": ("sbuf", [128, 4], "int32"),
+    "pf": ("sbuf", [128, 4], "float32"),
+    "it16": ("sbuf", [128, N * CD], "float32"),
+    "it4": ("sbuf", [128, CAP], "float32"),
+    "ithi": ("sbuf", [128, N * CD], "float32"),
+    "tri": ("sbuf", [128, N * CD], "float32"),
+    "rst": ("sbuf", [128, N * CD], "float32"),
+    "vc": ("sbuf", [128, N * CD], "float32"),
+    "hold": ("sbuf", [128, CAP], "float32"),
+    "inc": ("sbuf", [128, CAP], "float32"),
+    "neg": ("sbuf", [128, N * CD], "float32"),
+    "lm": ("sbuf", [128, N * CD], "float32"),
+    "cs": ("sbuf", [128, N * CD], "float32"),
+    "cloc": ("sbuf", [128, 2 * N], "uint16"),
+    "csend": ("sbuf", [128, 8], "uint16"),
+    "cown": ("sbuf", [128, 2], "uint16"),
+    "vb": ("sbuf", [128, N * CD + 8], "float32"),
+    "v": ("sbuf", [128, N * VW], "float32"),
+    "f": ("sbuf", [128, N * CAP], "float32"),
+    "a": ("sbuf", [128, N * CAP], "float32"),
+    "ai": ("sbuf", [128, N * 40], "int32"),
+    "aj": ("sbuf", [128, N * 40], "int32"),
+    "off": ("sbuf", [128, N * 40], "uint16"),
+    "xs": ("sbuf", [128, XW], "bfloat16"),
+    "h": ("sbuf", [128, N * 4 * CAP], "bfloat16"),
+    "qwb": ("sbuf", [128, 512], "bfloat16"),
+    "wq": ("sbuf", [128, 128], "float8_e4m3fn_x4"),
+    "wp": ("sbuf", [128, 128], "uint8"),
+    "q": ("sbuf", [128, N * CAP], "float8_e4m3fn_x4"),
+    "p": ("sbuf", [128, N * CAP], "uint8"),
+    "rc": ("sbuf", [128, N * CAP], "float8_e4m3fn_x4"),
+    "rp": ("sbuf", [128, N * CAP], "uint8"),
+    "cl": ("sbuf", [128, 8], "uint16"),
+    "m": ("sbuf", [128, MW], "float32"),
+    "z": ("sbuf", [128, MW], "float32"),
+    "ys": ("sbuf", [128, N * CD], "float32"),
+    "ps": ("psum", [128, 512 * N], "float32"),
+}
+SEMAPHORES = ["dc", "dr", "dx", "dq", "dy", "gi", "vv", "aa", "tt", "ls", "rq", "cc"] \
+    + ["co%d" % i for i in range(N)] + ["pl%d" % i for i in range(N)]
+
+
+def order_of(r, T, topo):
+    chip = [topo.chip(c) for c in T.cores]
+    mate = [[j for j in range(N) if topo.mates(chip[i], chip[j])][0] for i in range(N)]
+    plane = sorted([j for j in range(N) if topo.same_plane(chip[r], chip[j])], key=lambda j: (j - r) % N)
+    far = [mate[j] for j in plane]
+    o = []
+    for k in range(len(plane)):
+        o += [far[k], plane[len(plane) - 1 - k]]
+    return o + [mate[r]]
+
+
+def rank_program(g, core, T, topo):
+    rank = T.rank_of(core)
+    if rank is None:
+        return
+    op, act = AluOpType, ActivationFunctionType
+    V, A, E, Y = g.vector, g.scalar, g.tensor, g.sync
+    sem = T.sem
+    orders = [order_of(r, T, topo) for r in range(N)]
+    order = orders[rank]
+    pos_at = [orders[d].index(rank) if d != rank else None for d in range(N)]
+    src = [[r for r in range(N) if r != rank and orders[r][s] == rank][0] for s in range(S)]
+
+    def bits(es):
+        return sum(1 << e for e in es)
+    eng = [topo.engines(core, T.cores[d]) for d in order]
+    ids = []
+    for d in order:
+        a = topo.addr(T.cores[d])
+        ids.append(DstId(rid=a[0], pnc=a[1]))
+    share = [len(eng[0]) // 4] * 4 + [len(eng[0])]
+
+    vn, vw, an, tn, gn, ln_ = [0], [0], [0], [0], [0], [0]
+
+    def v(ins):
+        ins.then_inc(sem.vv, 1)
+        vn[0] += 1
+        return vn[0]
+
+    def vneed(n):
+        if n > vw[0]:
+            V.wait_ge(sem.vv, n)
+            vw[0] = n
+
+    def a_(ins):
+        ins.then_inc(sem.aa, 1)
+        an[0] += 1
+        return an[0]
+
+    def gi(ins):
+        ins.then_inc(sem.gi, 1)
+        gn[0] += 1
+        return gn[0]
+
+    for k in range(8):
+        (Y if k % 2 == 0 else A).dma_start(T.cdi[16 * k:16 * k + 16, 0:N], T.cd[:, :]).then_inc(sem.dc, 16)
+    Y.dma_start(T.raw[0:1, 0:ND], T.st[:, :]).then_inc(sem.dr, 16)
+    A.dma_start(T.raw[0:1, ND:2 * ND], T.ln[:, :]).then_inc(sem.dr, 16)
+    Y.dma_start(T.xs[:, 0:4 * TOK], T.x[:, :]).then_inc(sem.dx, 16)
+    A.dma_start(T.qwb[:, :], T.qw[:, :]).then_inc(sem.dq, 16)
+
+    g_ip = gi(g.iota(T.ip[:, 0:1], [[1, 1]], 0, 1))
+    gi(g.iota(T.it16[:, :], [[0, N], [1, CD]], 0, 0, allow_small_or_imprecise_dtypes=True))
+    gi(g.iota(T.ithi[:, :], [[HI, N * CD]], HI, 0, allow_small_or_imprecise_dtypes=True))
+    g_it = gi(g.iota(T.it4[:, :], [[0, CAP // 4], [1, 4]], 0, 0, allow_small_or_imprecise_dtypes=True))
+
+    v(V.memset(T.v[:, :], 0.0))
+    v(V.memset(T.inc[:, 0:1], 0.0))
+    v(V.memset(T.inc[:, 1:CAP], 4.0))
+    v(V.memset(T.neg[:, :], -BIG))
+    v(V.memset(T.vb[:, N * CD:N * CD + 8], 0.0))
+    V.wait_ge(sem.gi, g_it)
+    v(V.tensor_scalar(T.ii[:, 0:1], T.ip[:, 0:1], 15, None, op.bitwise_and))
+    v(V.tensor_scalar(T.ii[:, 1:2], T.ip[:, 0:1], 3, None, op.bitwise_and))
+    n = v(V.tensor_scalar(T.ii[:, 2:3], T.ip[:, 0:1], 15, 2, op.bitwise_and, op.logical_shift_right))
+    vneed(n)
+    n = v(V.tensor_copy(T.pf[:, 0:3], T.ii[:, 0:3]))
+    v(V.tensor_scalar(T.rst[:, :], T.it16[:, :], 1.0, None, op.min))
+    vneed(n)
+    v(V.tensor_scalar(T.tri[:, :], T.it16[:, :], T.pf[:, 0:1], None, op.is_le))
+    v(V.tensor_scalar(T.vc[:, :], T.ithi[:, :], T.pf[:, 1:2], None, op.add))
+    v_const = v(V.tensor_scalar(T.hold[:, :], T.it4[:, :], T.pf[:, 2:3], 1.0e9, op.is_le, op.mult))
+
+    V.wait_ge(sem.dc, 128)
+    v_cdu = v(V.tensor_copy(T.cdu[:, :], T.cdi[:, :]))
+    g.wait_ge(sem.vv, v_cdu)
+    g.remote_dma_fused([RemoteDMATransfer(
+        dst_ids=ids, dma_engine_mask=bits(eng[0]), remote_sem=sem.rq, srcs=[T.cdu[:, :]],
+        dsts=[T.cdl[:, N * pos_at[d]:N * pos_at[d] + N] for d in order])], local_sem=sem.ls)
+    ln_[0] += len(eng[0])
+    rq_total = sum(len(topo.engines(T.cores[d], core)) for d in order)
+
+    g.wait_ge(sem.dr, 32)
+    g_bc = gi(g.partition_broadcast(T.bc[:, :], T.raw[0:1, :], 128))
+
+    v_own = v(V.tensor_copy(T.cdown[:, 0:1], T.cdi[:, rank:rank + 1]))
+    v_pad = v(V.memset(T.xs[:, 4 * TOK:XW], 0.0))
+    v_m = v(V.memset(T.m[:, :], BIG))
+    v(V.memset(T.z[:, 0:1], 0.0))
+    v(V.memset(T.z[:, N * CAP + 1:MW], 0.0))
+    V.wait_ge(sem.gi, g_bc)
+    for u in range(ND // 16):
+        v(V.tensor_copy(T.tabl[:, 16 * u:16 * u + 16], T.bc[:, ND + u:2 * ND:ND // 16]))
+        n = v(V.tensor_scalar(T.tabs[:, 16 * u:16 * u + 16], T.bc[:, u:ND:ND // 16], 4.0, None, op.mult))
+    v_tab = n
+
+    def ends(lst, b, k):
+        lo, hi = CD * b, CD * (b + k)
+        n1 = v(V.tensor_tensor(T.lm[:, lo:hi], T.tabl[:, :].indirect(lst), T.tri[:, lo:hi], op.mult))
+        n2 = v(V.tensor_tensor(T.vb[:, lo:hi], T.tabs[:, :].indirect(lst), T.vc[:, lo:hi], op.add))
+        vneed(n1)
+        n3 = v(V.tensor_tensor_scan(T.cs[:, lo:hi], T.rst[:, lo:hi], T.lm[:, lo:hi], 0.0, op.mult, op.add))
+        vneed(n3)
+        n4 = v(V.tensor_copy(T.cloc[:, 2 * b:2 * (b + k):2], T.cs[:, lo + CD - 1:hi:CD]))
+        return n4
+
+    def ends_out(dst, b, k):
+        return v(V.tensor_scalar(dst, T.cs[:, CD * b + CD - 1:CD * (b + k):CD], float(CAP * rank), None, op.add))
+
+    def lists(s, between=None):
+        c = CAP * s
+        n = v(V.tensor_copy(T.v[:, VW * s:VW * (s + 1)].indirect(T.cloc[:, 2 * s:2 * s + 1]),
+                            T.vb[:, CD * s + 1:CD * (s + 1) + 1]))
+        if between is not None:
+            between()
+        vneed(n)
+        vneed(v(V.tensor_tensor_scan(T.f[:, c:c + CAP], T.inc[:, :], T.v[:, VW * s:VW * s + CAP],
+                                     T.vb[:, CD * s:CD * s + 1], op.add, op.max)))
+        vneed(v(V.tensor_tensor_scan(T.a[:, c:c + CAP], T.hold[:, :], T.f[:, c:c + CAP], 0.0, op.max, op.min)))
+        vneed(v(V.tensor_copy(T.ai[:, 40 * s:40 * s + 40], T.a[:, c + 3:c + CAP:4])))
+        vneed(v(V.tensor_scalar(T.aj[:, 40 * s:40 * s + 40], T.ai[:, 40 * s:40 * s + 40], HI - 1, None,
+                                op.bitwise_and)))
+        return v(V.tensor_copy(T.off[:, 40 * s:40 * s + 40], T.aj[:, 40 * s:40 * s + 40]))
+
+    a_w = [0]
+    def gather_a(s, n, lo=0, hi=40):
+        A.wait_ge(sem.vv, n)
+        return a_(A.activation(T.h[:, 4 * CAP * s + 16 * lo:4 * CAP * s + 16 * hi],
+                               T.xs[:, :].indirect(T.off[:, 40 * s + lo:40 * s + hi]), act.Copy))
+
+    def gather_v(s, n, lo, hi):
+        vneed(n)
+        return v(V.tensor_copy(T.h[:, 4 * CAP * s + 16 * lo:4 * CAP * s + 16 * hi],
+                               T.xs[:, :].indirect(T.off[:, 40 * s + lo:40 * s + hi])))
+
+    def quant(s, na, nv=0):
+        V.wait_ge(sem.aa, na)
+        vneed(nv)
+        return v(V.quantize_mx(T.q[:, CAP * s:CAP * (s + 1)], T.p[:, CAP * s:CAP * (s + 1)],
+                               T.h[:, 4 * CAP * s:4 * CAP * (s + 1)]))
+
+    vneed(v_tab)
+    n = ends(T.cdown[:, 0:1], S, 1)
+    v_cown = ends_out(T.cown[:, 0:1], S, 1)
+    vneed(n)
+    n = lists(S)
+    A.wait_ge(sem.dx, 16)
+    a_own = gather_a(S, n)
+    V.wait_ge(sem.dq, 16)
+    v_w = v(V.quantize_mx(T.wq[:, :], T.wp[:, :], T.qwb[:, :]))
+
+    V.wait_ge(sem.rq, rq_total)
+    vneed(v(V.tensor_copy(T.cdx[:, 0:S], T.cdl[:, rank:N * S:N])))
+    vneed(ends(T.cdx[:, 0:S], 0, S))
+
+    vs = [0]
+    def send_ends():
+        vs[0] = ends_out(T.csend[:, 0:S], 0, S)
+    V.wait_ge(sem.dx, 16)
+    v_q = [0] * N
+    n = lists(0, send_ends)
+    half = 20
+    a0 = gather_a(0, n, 0, half)
+    nv0 = gather_v(0, n, half, 40)
+    n1 = lists(1)
+    a1 = gather_a(1, n1)
+    v_q[S] = quant(S, a_own)
+    v_q[0] = quant(0, a0, nv0)
+    n2 = lists(2)
+    a2 = gather_a(2, n2)
+    v_q[1] = quant(1, a1)
+    n3 = lists(3)
+    a3 = gather_a(3, n3)
+    v_q[2] = quant(2, a2)
+    n4 = lists(4)
+    a4 = gather_a(4, n4, 0, half)
+    nv4 = gather_v(4, n4, half, 40)
+    v_q[3] = quant(3, a3)
+    v_q[4] = quant(4, a4, nv4)
+
+    def fused4(sm, pieces):
+        ts = []
+        for s in range(4):
+            es = eng[s][share[s] * s:share[s] * (s + 1)]
+            o, i = pieces(s)
+            ts.append(RemoteDMATransfer(dst_ids=[ids[s]], dma_engine_mask=bits(es), remote_sem=sm, srcs=[i], dsts=[o]))
+            ln_[0] += len(es)
+        g.remote_dma_fused(ts, local_sem=sem.ls)
+
+    def single(s, sm, o, i):
+        a = topo.addr(T.cores[order[s]])
+        g.remote_dma(o, i, remote_sem=sm, local_sem=sem.ls, pid=a[1], routing_id=a[0],
+                     dma_engine_mask=topo.mask(core, T.cores[order[s]]))
+        ln_[0] += len(eng[s])
+
+    land = slice(CAP * rank, CAP * (rank + 1))
+    g.wait_ge(sem.vv, vs[0])
+    fused4(sem.cc, lambda s: (T.cl[:, rank:rank + 1], T.csend[:, s:s + 1]))
+    single(4, sem.cc, T.cl[:, rank:rank + 1], T.csend[:, 4:5])
+
+    def codes(s):
+        g.wait_ge(sem.vv, v_q[s])
+        single(s, sem["co%d" % rank], T.rc[:, land].bitcast(dt.uint8),
+               T.q[:, CAP * s:CAP * (s + 1)].bitcast(dt.uint8))
+    for s in range(4):
+        codes(s)
+    fused4(sem["pl%d" % rank], lambda s: (T.rp[:, land], T.p[:, CAP * s:CAP * (s + 1)]))
+    codes(4)
+    single(4, sem["pl%d" % rank], T.rp[:, land], T.p[:, CAP * 4:CAP * 5])
+
+    def product(b, cq, cp, k):
+        E.matmul_mx(T.ps[:, 512 * b:512 * b + CAP], T.wq[:, :], T.wp[:, :], cq[:, k:k + CAP], cp[:, k:k + CAP],
+                    True, True).then_inc(sem.tt, 1)
+        tn[0] += 1
+        return tn[0]
+    E.wait_ge(sem.vv, v_q[S])
+    t_of = {rank: product(rank, T.q, T.p, CAP * S)}
+    for s in range(S):
+        d = src[s]
+        E.wait_ge(sem["co%d" % d], len(topo.engines(T.cores[d], core)))
+        E.wait_ge(sem["pl%d" % d], share[s])
+        t_of[d] = product(d, T.rc, T.rp, CAP * d)
+
+    V.wait_ge(sem.cc, sum(share))
+    vneed(v(V.tensor_copy(T.cl[:, rank:rank + 1], T.cown[:, 0:1])))
+    vneed(v(V.tensor_copy(T.m[:, :].indirect(T.cl[:, 0:N]), T.neg[:, :])))
+    for d in [rank] + src:
+        V.wait_ge(sem.tt, t_of[d])
+        n = v(V.tensor_tensor_scan(T.z[:, CAP * d + 1:CAP * (d + 1) + 1], T.m[:, CAP * d:CAP * (d + 1)],
+                                   T.ps[:, 512 * d:512 * d + CAP], -BIG, op.min, op.max))
+    vneed(n)
+    n = v(V.tensor_copy(T.ys[:, :], T.z[:, :].indirect(T.cl[:, 0:N])))
+    Y.wait_ge(sem.vv, n)
+    Y.dma_start(T.y[:, :], T.ys[:, :]).then_inc(sem.dy, 16)
+    Y.wait_ge(sem.dy, 16)
+    g.wait_ge(sem.ls, ln_[0])

@@ -6,9 +6,11 @@ N, CD, ND, TOK, CAP = 6, 16, 64, 768, 160
 S = N - 1
 VW = CAP + 8
 XW = 4 * (TOK + CAP)
+OW = 4 * CAP // 16
 HI = 4096
-MW = N * CAP + 8
 BIG = 1.0e29
+CUT = [26, 34, 34, 40, 20]
+OWN_AT = 3
 
 SCRATCH = {
     "cdi": ("sbuf", [128, N], "int32"),
@@ -31,19 +33,16 @@ SCRATCH = {
     "vc": ("sbuf", [128, N * CD], "float32"),
     "hold": ("sbuf", [128, CAP], "float32"),
     "inc": ("sbuf", [128, CAP], "float32"),
-    "neg": ("sbuf", [128, N * CD], "float32"),
+    "neg": ("sbuf", [128, CD], "float32"),
     "lm": ("sbuf", [128, N * CD], "float32"),
     "cs": ("sbuf", [128, N * CD], "float32"),
     "cloc": ("sbuf", [128, 2 * N], "uint16"),
-    "csend": ("sbuf", [128, 8], "uint16"),
-    "cown": ("sbuf", [128, 2], "uint16"),
     "vb": ("sbuf", [128, N * CD + 8], "float32"),
     "v": ("sbuf", [128, N * VW], "float32"),
     "f": ("sbuf", [128, N * CAP], "float32"),
-    "a": ("sbuf", [128, N * CAP], "float32"),
-    "ai": ("sbuf", [128, N * 40], "int32"),
-    "aj": ("sbuf", [128, N * 40], "int32"),
-    "off": ("sbuf", [128, N * 40], "uint16"),
+    "a": ("sbuf", [128, N * CAP], "int32"),
+    "aj": ("sbuf", [128, N * OW], "int32"),
+    "off": ("sbuf", [128, N * OW], "uint16"),
     "xs": ("sbuf", [128, XW], "bfloat16"),
     "h": ("sbuf", [128, N * 4 * CAP], "bfloat16"),
     "qwb": ("sbuf", [128, 512], "bfloat16"),
@@ -53,9 +52,9 @@ SCRATCH = {
     "p": ("sbuf", [128, N * CAP], "uint8"),
     "rc": ("sbuf", [128, N * CAP], "float8_e4m3fn_x4"),
     "rp": ("sbuf", [128, N * CAP], "uint8"),
-    "cl": ("sbuf", [128, 8], "uint16"),
-    "m": ("sbuf", [128, MW], "float32"),
-    "z": ("sbuf", [128, MW], "float32"),
+    "cl": ("sbuf", [128, 2 * N], "uint16"),
+    "m": ("sbuf", [128, N * VW], "float32"),
+    "z": ("sbuf", [128, N * VW], "float32"),
     "ys": ("sbuf", [128, N * CD], "float32"),
     "ps": ("psum", [128, 512 * N], "float32"),
 }
@@ -93,7 +92,8 @@ def rank_program(g, core, T, topo):
     for d in order:
         a = topo.addr(T.cores[d])
         ids.append(DstId(rid=a[0], pnc=a[1]))
-    share = [len(eng[0]) // 4] * 4 + [len(eng[0])]
+    ne = len(eng[0])
+    share = [ne // 4] * 4 + [ne]
 
     vn, vw, an, tn, gn, ln_ = [0], [0], [0], [0], [0], [0]
 
@@ -124,16 +124,15 @@ def rank_program(g, core, T, topo):
     Y.dma_start(T.xs[:, 0:4 * TOK], T.x[:, :]).then_inc(sem.dx, 16)
     A.dma_start(T.qwb[:, :], T.qw[:, :]).then_inc(sem.dq, 16)
 
-    g_ip = gi(g.iota(T.ip[:, 0:1], [[1, 1]], 0, 1))
+    gi(g.iota(T.ip[:, 0:1], [[1, 1]], 0, 1))
     gi(g.iota(T.it16[:, :], [[0, N], [1, CD]], 0, 0, allow_small_or_imprecise_dtypes=True))
     gi(g.iota(T.ithi[:, :], [[HI, N * CD]], HI, 0, allow_small_or_imprecise_dtypes=True))
     g_it = gi(g.iota(T.it4[:, :], [[0, CAP // 4], [1, 4]], 0, 0, allow_small_or_imprecise_dtypes=True))
 
-    v(V.memset(T.v[:, :], 0.0))
     v(V.memset(T.inc[:, 0:1], 0.0))
     v(V.memset(T.inc[:, 1:CAP], 4.0))
     v(V.memset(T.neg[:, :], -BIG))
-    v(V.memset(T.vb[:, N * CD:N * CD + 8], 0.0))
+    v(V.memset(T.vb[:, S * CD:N * CD + 8], 0.0))
     V.wait_ge(sem.gi, g_it)
     v(V.tensor_scalar(T.ii[:, 0:1], T.ip[:, 0:1], 15, None, op.bitwise_and))
     v(V.tensor_scalar(T.ii[:, 1:2], T.ip[:, 0:1], 3, None, op.bitwise_and))
@@ -144,7 +143,7 @@ def rank_program(g, core, T, topo):
     vneed(n)
     v(V.tensor_scalar(T.tri[:, :], T.it16[:, :], T.pf[:, 0:1], None, op.is_le))
     v(V.tensor_scalar(T.vc[:, :], T.ithi[:, :], T.pf[:, 1:2], None, op.add))
-    v_const = v(V.tensor_scalar(T.hold[:, :], T.it4[:, :], T.pf[:, 2:3], 1.0e9, op.is_le, op.mult))
+    v(V.tensor_scalar(T.hold[:, :], T.it4[:, :], T.pf[:, 2:3], 1.0e9, op.is_le, op.mult))
 
     V.wait_ge(sem.dc, 128)
     v_cdu = v(V.tensor_copy(T.cdu[:, :], T.cdi[:, :]))
@@ -152,115 +151,97 @@ def rank_program(g, core, T, topo):
     g.remote_dma_fused([RemoteDMATransfer(
         dst_ids=ids, dma_engine_mask=bits(eng[0]), remote_sem=sem.rq, srcs=[T.cdu[:, :]],
         dsts=[T.cdl[:, N * pos_at[d]:N * pos_at[d] + N] for d in order])], local_sem=sem.ls)
-    ln_[0] += len(eng[0])
+    ln_[0] += ne
     rq_total = sum(len(topo.engines(T.cores[d], core)) for d in order)
 
     g.wait_ge(sem.dr, 32)
     g_bc = gi(g.partition_broadcast(T.bc[:, :], T.raw[0:1, :], 128))
 
-    v_own = v(V.tensor_copy(T.cdown[:, 0:1], T.cdi[:, rank:rank + 1]))
-    v_pad = v(V.memset(T.xs[:, 4 * TOK:XW], 0.0))
+    v(V.tensor_copy(T.cdown[:, 0:1], T.cdi[:, rank:rank + 1]))
+    v_zero = v(V.memset(T.v[:, :], 0.0))
+    v(V.memset(T.xs[:, 4 * TOK:XW], 0.0))
     v_m = v(V.memset(T.m[:, :], BIG))
-    v(V.memset(T.z[:, 0:1], 0.0))
-    v(V.memset(T.z[:, N * CAP + 1:MW], 0.0))
+    A.wait_ge(sem.vv, v_zero)
+    a_z = a_(A.activation(T.z[:, :], T.v[:, :], act.Copy))
     V.wait_ge(sem.gi, g_bc)
     for u in range(ND // 16):
         v(V.tensor_copy(T.tabl[:, 16 * u:16 * u + 16], T.bc[:, ND + u:2 * ND:ND // 16]))
         n = v(V.tensor_scalar(T.tabs[:, 16 * u:16 * u + 16], T.bc[:, u:ND:ND // 16], 4.0, None, op.mult))
-    v_tab = n
+    V.wait_ge(sem.dq, 16)
+    v(V.quantize_mx(T.wq[:, :], T.wp[:, :], T.qwb[:, :]))
+    vneed(n)
 
     def ends(lst, b, k):
         lo, hi = CD * b, CD * (b + k)
         n1 = v(V.tensor_tensor(T.lm[:, lo:hi], T.tabl[:, :].indirect(lst), T.tri[:, lo:hi], op.mult))
-        n2 = v(V.tensor_tensor(T.vb[:, lo:hi], T.tabs[:, :].indirect(lst), T.vc[:, lo:hi], op.add))
+        v(V.tensor_tensor(T.vb[:, lo:hi], T.tabs[:, :].indirect(lst), T.vc[:, lo:hi], op.add))
         vneed(n1)
         n3 = v(V.tensor_tensor_scan(T.cs[:, lo:hi], T.rst[:, lo:hi], T.lm[:, lo:hi], 0.0, op.mult, op.add))
         vneed(n3)
-        n4 = v(V.tensor_copy(T.cloc[:, 2 * b:2 * (b + k):2], T.cs[:, lo + CD - 1:hi:CD]))
-        return n4
+        return v(V.tensor_copy(T.cloc[:, 2 * b:2 * (b + k):2], T.cs[:, lo + CD - 1:hi:CD]))
 
-    def ends_out(dst, b, k):
-        return v(V.tensor_scalar(dst, T.cs[:, CD * b + CD - 1:CD * (b + k):CD], float(CAP * rank), None, op.add))
-
-    def lists(s, between=None):
-        c = CAP * s
-        n = v(V.tensor_copy(T.v[:, VW * s:VW * (s + 1)].indirect(T.cloc[:, 2 * s:2 * s + 1]),
-                            T.vb[:, CD * s + 1:CD * (s + 1) + 1]))
-        if between is not None:
-            between()
-        vneed(n)
+    def lists(s):
+        c, o = CAP * s, slice(OW * s, OW * (s + 1))
+        vneed(v(V.tensor_copy(T.v[:, VW * s:VW * (s + 1)].indirect(T.cloc[:, 2 * s:2 * s + 1]),
+                              T.vb[:, CD * s + 1:CD * (s + 1) + 1])))
         vneed(v(V.tensor_tensor_scan(T.f[:, c:c + CAP], T.inc[:, :], T.v[:, VW * s:VW * s + CAP],
                                      T.vb[:, CD * s:CD * s + 1], op.add, op.max)))
         vneed(v(V.tensor_tensor_scan(T.a[:, c:c + CAP], T.hold[:, :], T.f[:, c:c + CAP], 0.0, op.max, op.min)))
-        vneed(v(V.tensor_copy(T.ai[:, 40 * s:40 * s + 40], T.a[:, c + 3:c + CAP:4])))
-        vneed(v(V.tensor_scalar(T.aj[:, 40 * s:40 * s + 40], T.ai[:, 40 * s:40 * s + 40], HI - 1, None,
-                                op.bitwise_and)))
-        return v(V.tensor_copy(T.off[:, 40 * s:40 * s + 40], T.aj[:, 40 * s:40 * s + 40]))
+        vneed(v(V.tensor_scalar(T.aj[:, o], T.a[:, c + 3:c + CAP:4], HI - 1, None, op.bitwise_and)))
+        return v(V.tensor_copy(T.off[:, o], T.aj[:, o]))
 
-    a_w = [0]
-    def gather_a(s, n, lo=0, hi=40):
-        A.wait_ge(sem.vv, n)
-        return a_(A.activation(T.h[:, 4 * CAP * s + 16 * lo:4 * CAP * s + 16 * hi],
-                               T.xs[:, :].indirect(T.off[:, 40 * s + lo:40 * s + hi]), act.Copy))
+    l_of, a_of, g_of, v_q = [0] * N, [0] * N, [0] * N, [0] * N
 
-    def gather_v(s, n, lo, hi):
-        vneed(n)
-        return v(V.tensor_copy(T.h[:, 4 * CAP * s + 16 * lo:4 * CAP * s + 16 * hi],
-                               T.xs[:, :].indirect(T.off[:, 40 * s + lo:40 * s + hi])))
+    def part(s, lo, hi):
+        return (T.h[:, 4 * CAP * s + 16 * lo:4 * CAP * s + 16 * hi],
+                T.xs[:, :].indirect(T.off[:, OW * s + lo:OW * s + hi]))
 
-    def quant(s, na, nv=0):
-        V.wait_ge(sem.aa, na)
-        vneed(nv)
-        return v(V.quantize_mx(T.q[:, CAP * s:CAP * (s + 1)], T.p[:, CAP * s:CAP * (s + 1)],
-                               T.h[:, 4 * CAP * s:4 * CAP * (s + 1)]))
+    def fetch_a(s, cut):
+        A.wait_ge(sem.vv, l_of[s])
+        o, i = part(s, 0, cut)
+        a_of[s] = a_(A.activation(o, i, act.Copy))
 
-    vneed(v_tab)
-    n = ends(T.cdown[:, 0:1], S, 1)
-    v_cown = ends_out(T.cown[:, 0:1], S, 1)
-    vneed(n)
-    n = lists(S)
+    def fetch_v(s, cut):
+        if cut < OW:
+            vneed(l_of[s])
+            o, i = part(s, cut, OW)
+            g_of[s] = v(V.tensor_copy(o, i))
+
+    def quant(s):
+        V.wait_ge(sem.aa, a_of[s])
+        vneed(g_of[s])
+        v_q[s] = v(V.quantize_mx(T.q[:, CAP * s:CAP * (s + 1)], T.p[:, CAP * s:CAP * (s + 1)],
+                                 T.h[:, 4 * CAP * s:4 * CAP * (s + 1)]))
+
     A.wait_ge(sem.dx, 16)
-    a_own = gather_a(S, n)
-    V.wait_ge(sem.dq, 16)
-    v_w = v(V.quantize_mx(T.wq[:, :], T.wp[:, :], T.qwb[:, :]))
-
+    V.wait_ge(sem.dx, 16)
+    V.wait_ge(sem.aa, a_z)
     V.wait_ge(sem.rq, rq_total)
     vneed(v(V.tensor_copy(T.cdx[:, 0:S], T.cdl[:, rank:N * S:N])))
-    vneed(ends(T.cdx[:, 0:S], 0, S))
+    v_ends = ends(T.cdx[:, 0:S], 0, S)
+    vneed(v_ends)
+    for s in range(S):
+        l_of[s] = lists(s)
+        fetch_a(s, CUT[s])
+        if s in (0, S - 1):
+            fetch_v(s, CUT[s])
+        if s > 0:
+            quant(s - 1)
+        if 0 < s < S - 1:
+            fetch_v(s, CUT[s])
+    quant(S - 1)
 
-    vs = [0]
-    def send_ends():
-        vs[0] = ends_out(T.csend[:, 0:S], 0, S)
-    V.wait_ge(sem.dx, 16)
-    v_q = [0] * N
-    n = lists(0, send_ends)
-    half = 20
-    a0 = gather_a(0, n, 0, half)
-    nv0 = gather_v(0, n, half, 40)
-    n1 = lists(1)
-    a1 = gather_a(1, n1)
-    v_q[S] = quant(S, a_own)
-    v_q[0] = quant(0, a0, nv0)
-    n2 = lists(2)
-    a2 = gather_a(2, n2)
-    v_q[1] = quant(1, a1)
-    n3 = lists(3)
-    a3 = gather_a(3, n3)
-    v_q[2] = quant(2, a2)
-    n4 = lists(4)
-    a4 = gather_a(4, n4, 0, half)
-    nv4 = gather_v(4, n4, half, 40)
-    v_q[3] = quant(3, a3)
-    v_q[4] = quant(4, a4, nv4)
+    vneed(ends(T.cdown[:, 0:1], S, 1))
+    l_of[S] = lists(S)
+    fetch_a(S, OW)
+    V.wait_ge(sem.cc, sum(share))
 
-    def fused4(sm, pieces):
-        ts = []
-        for s in range(4):
-            es = eng[s][share[s] * s:share[s] * (s + 1)]
-            o, i = pieces(s)
-            ts.append(RemoteDMATransfer(dst_ids=[ids[s]], dma_engine_mask=bits(es), remote_sem=sm, srcs=[i], dsts=[o]))
-            ln_[0] += len(es)
-        g.remote_dma_fused(ts, local_sem=sem.ls)
+    def ends_of(d):
+        return T.cloc[:, 2 * S:2 * S + 1] if d == rank else T.cl[:, 2 * d:2 * d + 1]
+    for d in range(N):
+        n = v(V.tensor_copy(T.m[:, VW * d:VW * (d + 1)].indirect(ends_of(d)), T.neg[:, 0:CD]))
+    quant(S)
+    vneed(n)
 
     def single(s, sm, o, i):
         a = topo.addr(T.cores[order[s]])
@@ -268,43 +249,55 @@ def rank_program(g, core, T, topo):
                      dma_engine_mask=topo.mask(core, T.cores[order[s]]))
         ln_[0] += len(eng[s])
 
-    land = slice(CAP * rank, CAP * (rank + 1))
-    g.wait_ge(sem.vv, vs[0])
-    fused4(sem.cc, lambda s: (T.cl[:, rank:rank + 1], T.csend[:, s:s + 1]))
-    single(4, sem.cc, T.cl[:, rank:rank + 1], T.csend[:, 4:5])
-
-    def codes(s):
-        g.wait_ge(sem.vv, v_q[s])
-        single(s, sem["co%d" % rank], T.rc[:, land].bitcast(dt.uint8),
-               T.q[:, CAP * s:CAP * (s + 1)].bitcast(dt.uint8))
+    my_end = T.cl[:, 2 * rank:2 * rank + 1]
+    g.wait_ge(sem.vv, v_ends)
+    ts = []
     for s in range(4):
-        codes(s)
-    fused4(sem["pl%d" % rank], lambda s: (T.rp[:, land], T.p[:, CAP * s:CAP * (s + 1)]))
-    codes(4)
-    single(4, sem["pl%d" % rank], T.rp[:, land], T.p[:, CAP * 4:CAP * 5])
+        es = eng[s][share[s] * s:share[s] * (s + 1)]
+        ts.append(RemoteDMATransfer(dst_ids=[ids[s]], dma_engine_mask=bits(es), remote_sem=sem.cc,
+                                    srcs=[T.cloc[:, 2 * s:2 * s + 1]], dsts=[my_end]))
+        ln_[0] += len(es)
+    g.remote_dma_fused(ts, local_sem=sem.ls)
+    single(4, sem.cc, my_end, T.cloc[:, 8:9])
+
+    land = slice(CAP * rank, CAP * (rank + 1))
+    for s in range(S):
+        mine = slice(CAP * s, CAP * (s + 1))
+        g.wait_ge(sem.vv, v_q[s])
+        single(s, sem["co%d" % rank], T.rc[:, land].bitcast(dt.uint8), T.q[:, mine].bitcast(dt.uint8))
+        single(s, sem["pl%d" % rank], T.rp[:, land], T.p[:, mine])
+
+    t_of = {}
 
     def product(b, cq, cp, k):
         E.matmul_mx(T.ps[:, 512 * b:512 * b + CAP], T.wq[:, :], T.wp[:, :], cq[:, k:k + CAP], cp[:, k:k + CAP],
                     True, True).then_inc(sem.tt, 1)
         tn[0] += 1
-        return tn[0]
-    E.wait_ge(sem.vv, v_q[S])
-    t_of = {rank: product(rank, T.q, T.p, CAP * S)}
-    for s in range(S):
-        d = src[s]
-        E.wait_ge(sem["co%d" % d], len(topo.engines(T.cores[d], core)))
-        E.wait_ge(sem["pl%d" % d], share[s])
-        t_of[d] = product(d, T.rc, T.rp, CAP * d)
+        t_of[b] = tn[0]
+    turn = src[:OWN_AT] + [rank] + src[OWN_AT:]
+    for d in turn:
+        if d == rank:
+            E.wait_ge(sem.vv, v_q[S])
+            product(rank, T.q, T.p, CAP * S)
+        else:
+            if not t_of:
+                E.wait_ge(sem.vv, v_q[0])
+            E.wait_ge(sem["co%d" % d], len(topo.engines(T.cores[d], core)))
+            E.wait_ge(sem["pl%d" % d], len(topo.engines(T.cores[d], core)))
+            product(d, T.rc, T.rp, CAP * d)
 
-    V.wait_ge(sem.cc, sum(share))
-    vneed(v(V.tensor_copy(T.cl[:, rank:rank + 1], T.cown[:, 0:1])))
-    vneed(v(V.tensor_copy(T.m[:, :].indirect(T.cl[:, 0:N]), T.neg[:, :])))
-    for d in [rank] + src:
+    for d in turn:
         V.wait_ge(sem.tt, t_of[d])
-        n = v(V.tensor_tensor_scan(T.z[:, CAP * d + 1:CAP * (d + 1) + 1], T.m[:, CAP * d:CAP * (d + 1)],
+        n = v(V.tensor_tensor_scan(T.z[:, VW * d + 1:VW * d + CAP + 1], T.m[:, VW * d:VW * d + CAP],
                                    T.ps[:, 512 * d:512 * d + CAP], -BIG, op.min, op.max))
-    vneed(n)
-    n = v(V.tensor_copy(T.ys[:, :], T.z[:, :].indirect(T.cl[:, 0:N])))
+        o, i = T.ys[:, CD * d:CD * (d + 1)], T.z[:, VW * d:VW * (d + 1)].indirect(ends_of(d))
+        if d != turn[-1]:
+            A.wait_ge(sem.vv, n)
+            a_(A.activation(o, i, act.Copy))
+        else:
+            vneed(n)
+            n = v(V.tensor_copy(o, i))
+    Y.wait_ge(sem.aa, an[0])
     Y.wait_ge(sem.vv, n)
     Y.dma_start(T.y[:, :], T.ys[:, :]).then_inc(sem.dy, 16)
     Y.wait_ge(sem.dy, 16)

@@ -9,8 +9,10 @@ XW = 4 * (TOK + CAP)
 OW = 4 * CAP // 16
 HI = 4096
 BIG = 1.0e29
-CUT = [26, 34, 34, 40, 20]
+CUT = [24, 34, 34, 34, 20, 40]
 OWN_AT = 3
+ORDER = ("s0 p0 s1 h0 p1 b0 s2 c0 h1 v0 b1 p2 c1 q0 s3 h2 v1 p3 b2 s4 c2 h3 q1 p4 b3 v2 c3 h4 q2 b4 v3 c4 v4 q3 q4 "
+         "s5 p5 h5 b5 c5 m q5").split()
 
 SCRATCH = {
     "cdi": ("sbuf", [128, N], "int32"),
@@ -35,8 +37,7 @@ SCRATCH = {
     "inc": ("sbuf", [128, CAP], "float32"),
     "neg": ("sbuf", [128, CD], "float32"),
     "lm": ("sbuf", [128, N * CD], "float32"),
-    "cs": ("sbuf", [128, N * CD], "float32"),
-    "cloc": ("sbuf", [128, 2 * N], "uint16"),
+    "cs": ("sbuf", [128, N * CD + 8], "uint16"),
     "vb": ("sbuf", [128, N * CD + 8], "float32"),
     "v": ("sbuf", [128, N * VW], "float32"),
     "f": ("sbuf", [128, N * CAP], "float32"),
@@ -160,7 +161,7 @@ def rank_program(g, core, T, topo):
     v(V.tensor_copy(T.cdown[:, 0:1], T.cdi[:, rank:rank + 1]))
     v_zero = v(V.memset(T.v[:, :], 0.0))
     v(V.memset(T.xs[:, 4 * TOK:XW], 0.0))
-    v_m = v(V.memset(T.m[:, :], BIG))
+    v(V.memset(T.m[:, :], BIG))
     A.wait_ge(sem.vv, v_zero)
     a_z = a_(A.activation(T.z[:, :], T.v[:, :], act.Copy))
     V.wait_ge(sem.gi, g_bc)
@@ -176,42 +177,15 @@ def rank_program(g, core, T, topo):
         n1 = v(V.tensor_tensor(T.lm[:, lo:hi], T.tabl[:, :].indirect(lst), T.tri[:, lo:hi], op.mult))
         v(V.tensor_tensor(T.vb[:, lo:hi], T.tabs[:, :].indirect(lst), T.vc[:, lo:hi], op.add))
         vneed(n1)
-        n3 = v(V.tensor_tensor_scan(T.cs[:, lo:hi], T.rst[:, lo:hi], T.lm[:, lo:hi], 0.0, op.mult, op.add))
-        vneed(n3)
-        return v(V.tensor_copy(T.cloc[:, 2 * b:2 * (b + k):2], T.cs[:, lo + CD - 1:hi:CD]))
+        return v(V.tensor_tensor_scan(T.cs[:, lo + 1:hi + 1], T.rst[:, lo:hi], T.lm[:, lo:hi], 0.0, op.mult, op.add))
 
-    def lists(s):
-        c, o = CAP * s, slice(OW * s, OW * (s + 1))
-        vneed(v(V.tensor_copy(T.v[:, VW * s:VW * (s + 1)].indirect(T.cloc[:, 2 * s:2 * s + 1]),
-                              T.vb[:, CD * s + 1:CD * (s + 1) + 1])))
-        vneed(v(V.tensor_tensor_scan(T.f[:, c:c + CAP], T.inc[:, :], T.v[:, VW * s:VW * s + CAP],
-                                     T.vb[:, CD * s:CD * s + 1], op.add, op.max)))
-        vneed(v(V.tensor_tensor_scan(T.a[:, c:c + CAP], T.hold[:, :], T.f[:, c:c + CAP], 0.0, op.max, op.min)))
-        vneed(v(V.tensor_scalar(T.aj[:, o], T.a[:, c + 3:c + CAP:4], HI - 1, None, op.bitwise_and)))
-        return v(V.tensor_copy(T.off[:, o], T.aj[:, o]))
+    def end_of(s):
+        return T.cs[:, CD * (s + 1):CD * (s + 1) + 1]
 
-    l_of, a_of, g_of, v_q = [0] * N, [0] * N, [0] * N, [0] * N
+    def places_of(d):
+        return end_of(S) if d == rank else T.cl[:, 2 * d:2 * d + 1]
 
-    def part(s, lo, hi):
-        return (T.h[:, 4 * CAP * s + 16 * lo:4 * CAP * s + 16 * hi],
-                T.xs[:, :].indirect(T.off[:, OW * s + lo:OW * s + hi]))
-
-    def fetch_a(s, cut):
-        A.wait_ge(sem.vv, l_of[s])
-        o, i = part(s, 0, cut)
-        a_of[s] = a_(A.activation(o, i, act.Copy))
-
-    def fetch_v(s, cut):
-        if cut < OW:
-            vneed(l_of[s])
-            o, i = part(s, cut, OW)
-            g_of[s] = v(V.tensor_copy(o, i))
-
-    def quant(s):
-        V.wait_ge(sem.aa, a_of[s])
-        vneed(g_of[s])
-        v_q[s] = v(V.quantize_mx(T.q[:, CAP * s:CAP * (s + 1)], T.p[:, CAP * s:CAP * (s + 1)],
-                                 T.h[:, 4 * CAP * s:4 * CAP * (s + 1)]))
+    n_own = ends(T.cdown[:, 0:1], S, 1)
 
     A.wait_ge(sem.dx, 16)
     V.wait_ge(sem.dx, 16)
@@ -219,29 +193,51 @@ def rank_program(g, core, T, topo):
     V.wait_ge(sem.rq, rq_total)
     vneed(v(V.tensor_copy(T.cdx[:, 0:S], T.cdl[:, rank:N * S:N])))
     v_ends = ends(T.cdx[:, 0:S], 0, S)
-    vneed(v_ends)
-    for s in range(S):
-        l_of[s] = lists(s)
-        fetch_a(s, CUT[s])
-        if s in (0, S - 1):
-            fetch_v(s, CUT[s])
-        if s > 0:
-            quant(s - 1)
-        if 0 < s < S - 1:
-            fetch_v(s, CUT[s])
-    quant(S - 1)
+    done, a_of, v_q = {}, {}, {}
 
-    vneed(ends(T.cdown[:, 0:1], S, 1))
-    l_of[S] = lists(S)
-    fetch_a(S, OW)
-    V.wait_ge(sem.cc, sum(share))
+    def part(s, lo, hi):
+        return (T.h[:, 4 * CAP * s + 16 * lo:4 * CAP * s + 16 * hi],
+                T.xs[:, :].indirect(T.off[:, OW * s + lo:OW * s + hi]))
 
-    def ends_of(d):
-        return T.cloc[:, 2 * S:2 * S + 1] if d == rank else T.cl[:, 2 * d:2 * d + 1]
-    for d in range(N):
-        n = v(V.tensor_copy(T.m[:, VW * d:VW * (d + 1)].indirect(ends_of(d)), T.neg[:, 0:CD]))
-    quant(S)
-    vneed(n)
+    for word in ORDER:
+        k = word[0]
+        s = int(word[1:] or 0)
+        c, w = slice(CAP * s, CAP * (s + 1)), slice(OW * s, OW * (s + 1))
+        last = done.get(s, 0)
+        if k == "s":
+            vneed(v_ends if s < S else n_own)
+            done[s] = v(V.tensor_copy(T.v[:, VW * s:VW * (s + 1)].indirect(end_of(s)),
+                                      T.vb[:, CD * s + 1:CD * (s + 1) + 1]))
+        elif k == "p":
+            vneed(last)
+            done[s] = v(V.tensor_tensor_scan(T.f[:, c], T.inc[:, :], T.v[:, VW * s:VW * s + CAP],
+                                             T.vb[:, CD * s:CD * s + 1], op.add, op.max))
+        elif k == "h":
+            vneed(last)
+            done[s] = v(V.tensor_tensor_scan(T.a[:, c], T.hold[:, :], T.f[:, c], 0.0, op.max, op.min))
+        elif k == "b":
+            vneed(last)
+            done[s] = v(V.tensor_scalar(T.aj[:, w], T.a[:, CAP * s + 3:CAP * (s + 1):4], HI - 1, None,
+                                        op.bitwise_and))
+        elif k == "c":
+            vneed(last)
+            done[s] = v(V.tensor_copy(T.off[:, w], T.aj[:, w]))
+            A.wait_ge(sem.vv, done[s])
+            o, i = part(s, 0, CUT[s])
+            a_of[s] = a_(A.activation(o, i, act.Copy))
+        elif k == "v":
+            vneed(last)
+            o, i = part(s, CUT[s], OW)
+            done[s] = v(V.tensor_copy(o, i))
+        elif k == "q":
+            V.wait_ge(sem.aa, a_of[s])
+            vneed(last)
+            v_q[s] = v(V.quantize_mx(T.q[:, c], T.p[:, c], T.h[:, 4 * CAP * s:4 * CAP * (s + 1)]))
+        else:
+            V.wait_ge(sem.cc, sum(share))
+            for d in range(N):
+                v_m = v(V.tensor_copy(T.m[:, VW * d:VW * (d + 1)].indirect(places_of(d)), T.neg[:, :]))
+    vneed(v_m)
 
     def single(s, sm, o, i):
         a = topo.addr(T.cores[order[s]])
@@ -255,10 +251,10 @@ def rank_program(g, core, T, topo):
     for s in range(4):
         es = eng[s][share[s] * s:share[s] * (s + 1)]
         ts.append(RemoteDMATransfer(dst_ids=[ids[s]], dma_engine_mask=bits(es), remote_sem=sem.cc,
-                                    srcs=[T.cloc[:, 2 * s:2 * s + 1]], dsts=[my_end]))
+                                    srcs=[end_of(s)], dsts=[my_end]))
         ln_[0] += len(es)
     g.remote_dma_fused(ts, local_sem=sem.ls)
-    single(4, sem.cc, my_end, T.cloc[:, 8:9])
+    single(4, sem.cc, my_end, end_of(4))
 
     land = slice(CAP * rank, CAP * (rank + 1))
     for s in range(S):
@@ -290,7 +286,7 @@ def rank_program(g, core, T, topo):
         V.wait_ge(sem.tt, t_of[d])
         n = v(V.tensor_tensor_scan(T.z[:, VW * d + 1:VW * d + CAP + 1], T.m[:, VW * d:VW * d + CAP],
                                    T.ps[:, 512 * d:512 * d + CAP], -BIG, op.min, op.max))
-        o, i = T.ys[:, CD * d:CD * (d + 1)], T.z[:, VW * d:VW * (d + 1)].indirect(ends_of(d))
+        o, i = T.ys[:, CD * d:CD * (d + 1)], T.z[:, VW * d:VW * (d + 1)].indirect(places_of(d))
         if d != turn[-1]:
             A.wait_ge(sem.vv, n)
             a_(A.activation(o, i, act.Copy))

@@ -7,42 +7,46 @@ S = N - 1
 VW = CAP + 8
 XW = 4 * (TOK + CAP)
 OW = 4 * CAP // 16
-HI = 4096
+RAMP = 4096
 BIG = 1.0e29
-CUT = [24, 34, 34, 34, 20, 40]
+LISTS = [(0, 1), (1, S), (S, N)]
+CUT = [24, 26, 32, 28, 32, 40]
 OWN_AT = 3
-ORDER = ("s0 p0 s1 h0 p1 b0 s2 c0 h1 v0 b1 p2 c1 q0 s3 h2 v1 p3 b2 s4 c2 h3 q1 p4 b3 v2 c3 h4 q2 b4 v3 c4 v4 q3 q4 "
-         "s5 p5 h5 b5 c5 m q5").split()
+EARLY = "l2 g2 e2 n2 d2".split()
+ORDER = ("i g0 l0 e0 g1 n0 d0 e1 l1 s0 d1 n1 p0 s1 s3 h0 s2 p1 c0 p2 h1 v0 c1 h2 p3 q0 c2 v1 s4 h3 q1 p4 c3 v2 h4 s5 "
+         "q2 c4 v3 p5 q3 h5 v4 c5 q4 m q5").split()
 
 SCRATCH = {
     "cdi": ("sbuf", [128, N], "int32"),
     "cdu": ("sbuf", [128, N], "uint16"),
-    "cdl": ("sbuf", [128, N * S], "uint16"),
-    "cdx": ("sbuf", [128, 8], "uint16"),
+    "cdl": ("sbuf", [128, N * S + 2], "uint16"),
+    "cdx": ("sbuf", [128, 4], "uint16"),
     "cdown": ("sbuf", [128, 2], "uint16"),
     "raw": ("sbuf", [128, 2 * ND], "int32"),
     "bc": ("sbuf", [128, 2 * ND], "int32"),
     "tabs": ("sbuf", [128, ND], "float32"),
     "tabl": ("sbuf", [128, ND], "float32"),
+    "tabm": ("sbuf", [128, ND], "float32"),
+    "tabe": ("sbuf", [128, ND], "float32"),
     "ip": ("sbuf", [128, 1], "int32"),
     "ii": ("sbuf", [128, 4], "int32"),
     "pf": ("sbuf", [128, 4], "float32"),
     "it16": ("sbuf", [128, N * CD], "float32"),
     "it4": ("sbuf", [128, CAP], "float32"),
-    "ithi": ("sbuf", [128, N * CD], "float32"),
+    "itr": ("sbuf", [128, CAP], "float32"),
     "tri": ("sbuf", [128, N * CD], "float32"),
     "rst": ("sbuf", [128, N * CD], "float32"),
-    "vc": ("sbuf", [128, N * CD], "float32"),
     "hold": ("sbuf", [128, CAP], "float32"),
     "inc": ("sbuf", [128, CAP], "float32"),
     "neg": ("sbuf", [128, CD], "float32"),
     "lm": ("sbuf", [128, N * CD], "float32"),
     "cs": ("sbuf", [128, N * CD + 8], "uint16"),
-    "vb": ("sbuf", [128, N * CD + 8], "float32"),
+    "sg": ("sbuf", [128, N * CD], "float32"),
+    "eg": ("sbuf", [128, N * CD + 8], "float32"),
+    "dg": ("sbuf", [128, N * CD + 8], "float32"),
     "v": ("sbuf", [128, N * VW], "float32"),
     "f": ("sbuf", [128, N * CAP], "float32"),
-    "a": ("sbuf", [128, N * CAP], "int32"),
-    "aj": ("sbuf", [128, N * OW], "int32"),
+    "a": ("sbuf", [128, N * CAP], "float32"),
     "off": ("sbuf", [128, N * OW], "uint16"),
     "xs": ("sbuf", [128, XW], "bfloat16"),
     "h": ("sbuf", [128, N * 4 * CAP], "bfloat16"),
@@ -127,31 +131,33 @@ def rank_program(g, core, T, topo):
 
     gi(g.iota(T.ip[:, 0:1], [[1, 1]], 0, 1))
     gi(g.iota(T.it16[:, :], [[0, N], [1, CD]], 0, 0, allow_small_or_imprecise_dtypes=True))
-    gi(g.iota(T.ithi[:, :], [[HI, N * CD]], HI, 0, allow_small_or_imprecise_dtypes=True))
     g_it = gi(g.iota(T.it4[:, :], [[0, CAP // 4], [1, 4]], 0, 0, allow_small_or_imprecise_dtypes=True))
 
-    v(V.memset(T.inc[:, 0:1], 0.0))
-    v(V.memset(T.inc[:, 1:CAP], 4.0))
     v(V.memset(T.neg[:, :], -BIG))
-    v(V.memset(T.vb[:, S * CD:N * CD + 8], 0.0))
+    v(V.memset(T.dg[:, :], 0.0))
     V.wait_ge(sem.gi, g_it)
     v(V.tensor_scalar(T.ii[:, 0:1], T.ip[:, 0:1], 15, None, op.bitwise_and))
     v(V.tensor_scalar(T.ii[:, 1:2], T.ip[:, 0:1], 3, None, op.bitwise_and))
     n = v(V.tensor_scalar(T.ii[:, 2:3], T.ip[:, 0:1], 15, 2, op.bitwise_and, op.logical_shift_right))
+    n2 = v(V.tensor_scalar(T.itr[:, :], T.it4[:, :], 1.0, 4.0 * RAMP, op.min, op.mult))
     vneed(n)
     n = v(V.tensor_copy(T.pf[:, 0:3], T.ii[:, 0:3]))
     v(V.tensor_scalar(T.rst[:, :], T.it16[:, :], 1.0, None, op.min))
+    vneed(n2)
+    n2 = v(V.tensor_scalar(T.inc[:, :], T.itr[:, :], 4.0 - 3 * RAMP, None, op.add))
     vneed(n)
     v(V.tensor_scalar(T.tri[:, :], T.it16[:, :], T.pf[:, 0:1], None, op.is_le))
-    v(V.tensor_scalar(T.vc[:, :], T.ithi[:, :], T.pf[:, 1:2], None, op.add))
+    v(V.tensor_scalar(T.pf[:, 3:4], T.pf[:, 2:3], float(RAMP), T.pf[:, 1:2], op.mult, op.subtract))
     v(V.tensor_scalar(T.hold[:, :], T.it4[:, :], T.pf[:, 2:3], 1.0e9, op.is_le, op.mult))
+    vneed(n2)
+    v(V.memset(T.inc[:, 0:1], 0.0))
 
     V.wait_ge(sem.dc, 128)
     v_cdu = v(V.tensor_copy(T.cdu[:, :], T.cdi[:, :]))
     g.wait_ge(sem.vv, v_cdu)
     g.remote_dma_fused([RemoteDMATransfer(
         dst_ids=ids, dma_engine_mask=bits(eng[0]), remote_sem=sem.rq, srcs=[T.cdu[:, :]],
-        dsts=[T.cdl[:, N * pos_at[d]:N * pos_at[d] + N] for d in order])], local_sem=sem.ls)
+        dsts=[T.cdl[:, N * pos_at[d] + d % 2:N * pos_at[d] + d % 2 + N] for d in order])], local_sem=sem.ls)
     ln_[0] += ne
     rq_total = sum(len(topo.engines(T.cores[d], core)) for d in order)
 
@@ -168,16 +174,12 @@ def rank_program(g, core, T, topo):
     for u in range(ND // 16):
         v(V.tensor_copy(T.tabl[:, 16 * u:16 * u + 16], T.bc[:, ND + u:2 * ND:ND // 16]))
         n = v(V.tensor_scalar(T.tabs[:, 16 * u:16 * u + 16], T.bc[:, u:ND:ND // 16], 4.0, None, op.mult))
+    vneed(n)
+    n = v(V.tensor_scalar(T.tabm[:, :], T.tabl[:, :], 4.0, None, op.mult))
     V.wait_ge(sem.dq, 16)
     v(V.quantize_mx(T.wq[:, :], T.wp[:, :], T.qwb[:, :]))
     vneed(n)
-
-    def ends(lst, b, k):
-        lo, hi = CD * b, CD * (b + k)
-        n1 = v(V.tensor_tensor(T.lm[:, lo:hi], T.tabl[:, :].indirect(lst), T.tri[:, lo:hi], op.mult))
-        v(V.tensor_tensor(T.vb[:, lo:hi], T.tabs[:, :].indirect(lst), T.vc[:, lo:hi], op.add))
-        vneed(n1)
-        return v(V.tensor_tensor_scan(T.cs[:, lo + 1:hi + 1], T.rst[:, lo:hi], T.lm[:, lo:hi], 0.0, op.mult, op.add))
+    vneed(v(V.tensor_tensor(T.tabe[:, :], T.tabs[:, :], T.tabm[:, :], op.add)))
 
     def end_of(s):
         return T.cs[:, CD * (s + 1):CD * (s + 1) + 1]
@@ -185,59 +187,79 @@ def rank_program(g, core, T, topo):
     def places_of(d):
         return end_of(S) if d == rank else T.cl[:, 2 * d:2 * d + 1]
 
-    n_own = ends(T.cdown[:, 0:1], S, 1)
-
-    A.wait_ge(sem.dx, 16)
-    V.wait_ge(sem.dx, 16)
-    V.wait_ge(sem.aa, a_z)
-    V.wait_ge(sem.rq, rq_total)
-    vneed(v(V.tensor_copy(T.cdx[:, 0:S], T.cdl[:, rank:N * S:N])))
-    v_ends = ends(T.cdx[:, 0:S], 0, S)
-    done, a_of, v_q = {}, {}, {}
+    first = rank + rank % 2
+    numbers = [T.cdl[:, first:first + 1], T.cdx[:, 0:S - 1], T.cdown[:, 0:1]]
 
     def part(s, lo, hi):
         return (T.h[:, 4 * CAP * s + 16 * lo:4 * CAP * s + 16 * hi],
                 T.xs[:, :].indirect(T.off[:, OW * s + lo:OW * s + hi]))
 
-    for word in ORDER:
+    at, a_of = {}, {}
+
+    def work(word):
         k = word[0]
         s = int(word[1:] or 0)
         c, w = slice(CAP * s, CAP * (s + 1)), slice(OW * s, OW * (s + 1))
-        last = done.get(s, 0)
-        if k == "s":
-            vneed(v_ends if s < S else n_own)
-            done[s] = v(V.tensor_copy(T.v[:, VW * s:VW * (s + 1)].indirect(end_of(s)),
-                                      T.vb[:, CD * s + 1:CD * (s + 1) + 1]))
+        if k == "i":
+            b = first + N
+            x = v(V.tensor_copy(T.cdx[:, 0:S - 1], T.cdl[:, b:b + N * (S - 2) + 1:N]))
+        elif k in "lgend":
+            lo, hi = CD * LISTS[s][0], CD * LISTS[s][1]
+            if k in "lge" and s == 1:
+                vneed(at["i"])
+            if k == "l":
+                x = v(V.tensor_tensor(T.lm[:, lo:hi], T.tabl[:, :].indirect(numbers[s]), T.tri[:, lo:hi], op.mult))
+            elif k == "g":
+                x = v(V.tensor_copy(T.sg[:, lo:hi], T.tabs[:, :].indirect(numbers[s])))
+            elif k == "e":
+                x = v(V.tensor_copy(T.eg[:, lo + 1:hi + 1], T.tabe[:, :].indirect(numbers[s])))
+            elif k == "n":
+                vneed(at["l%d" % s])
+                x = v(V.tensor_tensor_scan(T.cs[:, lo + 1:hi + 1], T.rst[:, lo:hi], T.lm[:, lo:hi], 0.0,
+                                           op.mult, op.add))
+            else:
+                vneed(max(at["g%d" % s], at["e%d" % s]))
+                x = v(V.tensor_tensor(T.dg[:, lo + 1:hi], T.sg[:, lo + 1:hi], T.eg[:, lo + 1:hi], op.subtract))
+        elif k == "s":
+            b = 0 if s == 0 else 2 if s == S else 1
+            vneed(max(at["n%d" % b], at["d%d" % b]))
+            x = v(V.tensor_copy(T.v[:, VW * s:VW * (s + 1)].indirect(end_of(s)), T.dg[:, CD * s + 1:CD * (s + 1) + 1]))
         elif k == "p":
-            vneed(last)
-            done[s] = v(V.tensor_tensor_scan(T.f[:, c], T.inc[:, :], T.v[:, VW * s:VW * s + CAP],
-                                             T.vb[:, CD * s:CD * s + 1], op.add, op.max))
+            vneed(at["s%d" % s])
+            x = v(V.tensor_tensor_scan(T.f[:, c], T.inc[:, :], T.v[:, VW * s:VW * s + CAP],
+                                       T.sg[:, CD * s:CD * s + 1], op.add, op.add))
         elif k == "h":
-            vneed(last)
-            done[s] = v(V.tensor_tensor_scan(T.a[:, c], T.hold[:, :], T.f[:, c], 0.0, op.max, op.min))
-        elif k == "b":
-            vneed(last)
-            done[s] = v(V.tensor_scalar(T.aj[:, w], T.a[:, CAP * s + 3:CAP * (s + 1):4], HI - 1, None,
-                                        op.bitwise_and))
+            vneed(at["p%d" % s])
+            x = v(V.tensor_tensor_scan(T.a[:, c], T.hold[:, :], T.f[:, c], 0.0, op.max, op.min))
         elif k == "c":
-            vneed(last)
-            done[s] = v(V.tensor_copy(T.off[:, w], T.aj[:, w]))
-            A.wait_ge(sem.vv, done[s])
+            vneed(at["h%d" % s])
+            x = v(V.tensor_scalar(T.off[:, w], T.a[:, CAP * s + 3:CAP * (s + 1):4], T.pf[:, 3:4], None, op.subtract))
+            A.wait_ge(sem.vv, x)
             o, i = part(s, 0, CUT[s])
             a_of[s] = a_(A.activation(o, i, act.Copy))
         elif k == "v":
-            vneed(last)
+            vneed(at["c%d" % s])
             o, i = part(s, CUT[s], OW)
-            done[s] = v(V.tensor_copy(o, i))
+            x = v(V.tensor_copy(o, i))
         elif k == "q":
             V.wait_ge(sem.aa, a_of[s])
-            vneed(last)
-            v_q[s] = v(V.quantize_mx(T.q[:, c], T.p[:, c], T.h[:, 4 * CAP * s:4 * CAP * (s + 1)]))
+            vneed(at.get("v%d" % s, 0))
+            x = v(V.quantize_mx(T.q[:, c], T.p[:, c], T.h[:, 4 * CAP * s:4 * CAP * (s + 1)]))
         else:
             V.wait_ge(sem.cc, sum(share))
             for d in range(N):
-                v_m = v(V.tensor_copy(T.m[:, VW * d:VW * (d + 1)].indirect(places_of(d)), T.neg[:, :]))
-    vneed(v_m)
+                x = v(V.tensor_copy(T.m[:, VW * d:VW * (d + 1)].indirect(places_of(d)), T.neg[:, :]))
+        at[word] = x
+
+    for word in EARLY:
+        work(word)
+    A.wait_ge(sem.dx, 16)
+    V.wait_ge(sem.dx, 16)
+    V.wait_ge(sem.aa, a_z)
+    V.wait_ge(sem.rq, rq_total)
+    for word in ORDER:
+        work(word)
+    vneed(at["m"])
 
     def single(s, sm, o, i):
         a = topo.addr(T.cores[order[s]])
@@ -246,7 +268,7 @@ def rank_program(g, core, T, topo):
         ln_[0] += len(eng[s])
 
     my_end = T.cl[:, 2 * rank:2 * rank + 1]
-    g.wait_ge(sem.vv, v_ends)
+    g.wait_ge(sem.vv, max(at["n0"], at["n1"]))
     ts = []
     for s in range(4):
         es = eng[s][share[s] * s:share[s] * (s + 1)]
@@ -259,7 +281,7 @@ def rank_program(g, core, T, topo):
     land = slice(CAP * rank, CAP * (rank + 1))
     for s in range(S):
         mine = slice(CAP * s, CAP * (s + 1))
-        g.wait_ge(sem.vv, v_q[s])
+        g.wait_ge(sem.vv, at["q%d" % s])
         single(s, sem["co%d" % rank], T.rc[:, land].bitcast(dt.uint8), T.q[:, mine].bitcast(dt.uint8))
         single(s, sem["pl%d" % rank], T.rp[:, land], T.p[:, mine])
 
@@ -273,11 +295,11 @@ def rank_program(g, core, T, topo):
     turn = src[:OWN_AT] + [rank] + src[OWN_AT:]
     for d in turn:
         if d == rank:
-            E.wait_ge(sem.vv, v_q[S])
+            E.wait_ge(sem.vv, at["q%d" % S])
             product(rank, T.q, T.p, CAP * S)
         else:
             if not t_of:
-                E.wait_ge(sem.vv, v_q[0])
+                E.wait_ge(sem.vv, at["q0"])
             E.wait_ge(sem["co%d" % d], len(topo.engines(T.cores[d], core)))
             E.wait_ge(sem["pl%d" % d], len(topo.engines(T.cores[d], core)))
             product(d, T.rc, T.rp, CAP * d)

import numpy as np
from concourse.bass import DstId, RemoteDMATransfer
from concourse.mybir import dt, AluOpType, ActivationFunctionType

N, CD, ND, TOK, CAP = 6, 16, 64, 768, 160
S = N - 1
VW = CAP + 8
XW = 4 * (TOK + CAP)
OW = 4 * CAP // 16
RAMP = 4096
BIG = 1.0e29
LISTS = [(0, 1), (1, S), (S, N)]
CUT = [24, 26, 32, 28, 32, 40]
OWN_AT = 3
EARLY = "l2 g2 e2 n2 d2".split()
ORDER = ("i g0 l0 e0 g1 n0 d0 e1 l1 s0 d1 n1 p0 s1 s3 h0 s2 p1 c0 p2 h1 v0 c1 h2 p3 q0 c2 v1 s4 h3 q1 p4 c3 v2 h4 s5 "
         "q2 c4 v3 p5 q3 h5 v4 c5 q4 m q5").split()

SCRATCH = {
    "cdi": ("sbuf", [128, N], "int32"),
    "cdu": ("sbuf", [128, N], "uint16"),
    "cdl": ("sbuf", [128, N * S + 2], "uint16"),
    "cdx": ("sbuf", [128, 4], "uint16"),
    "cdown": ("sbuf", [128, 2], "uint16"),
    "raw": ("sbuf", [128, 2 * ND], "int32"),
    "bc": ("sbuf", [128, 2 * ND], "int32"),
    "tabs": ("sbuf", [128, ND], "float32"),
    "tabl": ("sbuf", [128, ND], "float32"),
    "tabm": ("sbuf", [128, ND], "float32"),
    "tabe": ("sbuf", [128, ND], "float32"),
    "ip": ("sbuf", [128, 1], "int32"),
    "ii": ("sbuf", [128, 4], "int32"),
    "pf": ("sbuf", [128, 4], "float32"),
    "it16": ("sbuf", [128, N * CD], "float32"),
    "it4": ("sbuf", [128, CAP], "float32"),
    "itr": ("sbuf", [128, CAP], "float32"),
    "tri": ("sbuf", [128, N * CD], "float32"),
    "rst": ("sbuf", [128, N * CD], "float32"),
    "hold": ("sbuf", [128, CAP], "float32"),
    "inc": ("sbuf", [128, CAP], "float32"),
    "neg": ("sbuf", [128, CD], "float32"),
    "lm": ("sbuf", [128, N * CD], "float32"),
    "cs": ("sbuf", [128, N * CD + 8], "uint16"),
    "sg": ("sbuf", [128, N * CD], "float32"),
    "eg": ("sbuf", [128, N * CD + 8], "float32"),
    "dg": ("sbuf", [128, N * CD + 8], "float32"),
    "v": ("sbuf", [128, N * VW], "float32"),
    "f": ("sbuf", [128, N * CAP], "float32"),
    "a": ("sbuf", [128, N * CAP], "float32"),
    "off": ("sbuf", [128, N * OW], "uint16"),
    "xs": ("sbuf", [128, XW], "bfloat16"),
    "h": ("sbuf", [128, N * 4 * CAP], "bfloat16"),
    "qwb": ("sbuf", [128, 512], "bfloat16"),
    "wq": ("sbuf", [128, 128], "float8_e4m3fn_x4"),
    "wp": ("sbuf", [128, 128], "uint8"),
    "q": ("sbuf", [128, N * CAP], "float8_e4m3fn_x4"),
    "p": ("sbuf", [128, N * CAP], "uint8"),
    "rc": ("sbuf", [128, N * CAP], "float8_e4m3fn_x4"),
    "rp": ("sbuf", [128, N * CAP], "uint8"),
    "cl": ("sbuf", [128, 2 * N], "uint16"),
    "m": ("sbuf", [128, N * VW], "float32"),
    "z": ("sbuf", [128, N * VW], "float32"),
    "ys": ("sbuf", [128, N * CD], "float32"),
    "ps": ("psum", [128, 512 * N], "float32"),
}
SEMAPHORES = ["dc", "dr", "dx", "dq", "dy", "gi", "vv", "aa", "tt", "ls", "rq", "cc"] \
    + ["co%d" % i for i in range(N)] + ["pl%d" % i for i in range(N)]


def order_of(r, T, topo):
    chip = [topo.chip(c) for c in T.cores]
    mate = [[j for j in range(N) if topo.mates(chip[i], chip[j])][0] for i in range(N)]
    plane = sorted([j for j in range(N) if topo.same_plane(chip[r], chip[j])], key=lambda j: (j - r) % N)
    far = [mate[j] for j in plane]
    o = []
    for k in range(len(plane)):
        o += [far[k], plane[len(plane) - 1 - k]]
    return o + [mate[r]]


def rank_program(g, core, T, topo):
    rank = T.rank_of(core)
    if rank is None:
        return
    op, act = AluOpType, ActivationFunctionType
    V, A, E, Y = g.vector, g.scalar, g.tensor, g.sync
    sem = T.sem
    orders = [order_of(r, T, topo) for r in range(N)]
    order = orders[rank]
    pos_at = [orders[d].index(rank) if d != rank else None for d in range(N)]
    src = [[r for r in range(N) if r != rank and orders[r][s] == rank][0] for s in range(S)]

    def bits(es):
        return sum(1 << e for e in es)
    eng = [topo.engines(core, T.cores[d]) for d in order]
    ids = []
    for d in order:
        a = topo.addr(T.cores[d])
        ids.append(DstId(rid=a[0], pnc=a[1]))
    ne = len(eng[0])
    share = [ne // 4] * 4 + [ne]

    vn, vw, an, tn, gn, ln_ = [0], [0], [0], [0], [0], [0]

    def v(ins):
        ins.then_inc(sem.vv, 1)
        vn[0] += 1
        return vn[0]

    def vneed(n):
        if n > vw[0]:
            V.wait_ge(sem.vv, n)
            vw[0] = n

    def a_(ins):
        ins.then_inc(sem.aa, 1)
        an[0] += 1
        return an[0]

    def gi(ins):
        ins.then_inc(sem.gi, 1)
        gn[0] += 1
        return gn[0]

    for k in range(8):
        (Y if k % 2 == 0 else A).dma_start(T.cdi[16 * k:16 * k + 16, 0:N], T.cd[:, :]).then_inc(sem.dc, 16)
    Y.dma_start(T.raw[0:1, 0:ND], T.st[:, :]).then_inc(sem.dr, 16)
    A.dma_start(T.raw[0:1, ND:2 * ND], T.ln[:, :]).then_inc(sem.dr, 16)
    Y.dma_start(T.xs[:, 0:4 * TOK], T.x[:, :]).then_inc(sem.dx, 16)
    A.dma_start(T.qwb[:, :], T.qw[:, :]).then_inc(sem.dq, 16)

    gi(g.iota(T.ip[:, 0:1], [[1, 1]], 0, 1))
    gi(g.iota(T.it16[:, :], [[0, N], [1, CD]], 0, 0, allow_small_or_imprecise_dtypes=True))
    g_it = gi(g.iota(T.it4[:, :], [[0, CAP // 4], [1, 4]], 0, 0, allow_small_or_imprecise_dtypes=True))

    v(V.memset(T.neg[:, :], -BIG))
    v(V.memset(T.dg[:, :], 0.0))
    V.wait_ge(sem.gi, g_it)
    v(V.tensor_scalar(T.ii[:, 0:1], T.ip[:, 0:1], 15, None, op.bitwise_and))
    v(V.tensor_scalar(T.ii[:, 1:2], T.ip[:, 0:1], 3, None, op.bitwise_and))
    n = v(V.tensor_scalar(T.ii[:, 2:3], T.ip[:, 0:1], 15, 2, op.bitwise_and, op.logical_shift_right))
    n2 = v(V.tensor_scalar(T.itr[:, :], T.it4[:, :], 1.0, 4.0 * RAMP, op.min, op.mult))
    vneed(n)
    n = v(V.tensor_copy(T.pf[:, 0:3], T.ii[:, 0:3]))
    v(V.tensor_scalar(T.rst[:, :], T.it16[:, :], 1.0, None, op.min))
    vneed(n2)
    n2 = v(V.tensor_scalar(T.inc[:, :], T.itr[:, :], 4.0 - 3 * RAMP, None, op.add))
    vneed(n)
    v(V.tensor_scalar(T.tri[:, :], T.it16[:, :], T.pf[:, 0:1], None, op.is_le))
    v(V.tensor_scalar(T.pf[:, 3:4], T.pf[:, 2:3], float(RAMP), T.pf[:, 1:2], op.mult, op.subtract))
    v(V.tensor_scalar(T.hold[:, :], T.it4[:, :], T.pf[:, 2:3], 1.0e9, op.is_le, op.mult))
    vneed(n2)
    v(V.memset(T.inc[:, 0:1], 0.0))

    V.wait_ge(sem.dc, 128)
    v_cdu = v(V.tensor_copy(T.cdu[:, :], T.cdi[:, :]))
    g.wait_ge(sem.vv, v_cdu)
    g.remote_dma_fused([RemoteDMATransfer(
        dst_ids=ids, dma_engine_mask=bits(eng[0]), remote_sem=sem.rq, srcs=[T.cdu[:, :]],
        dsts=[T.cdl[:, N * pos_at[d] + d % 2:N * pos_at[d] + d % 2 + N] for d in order])], local_sem=sem.ls)
    ln_[0] += ne
    rq_total = sum(len(topo.engines(T.cores[d], core)) for d in order)

    g.wait_ge(sem.dr, 32)
    g_bc = gi(g.partition_broadcast(T.bc[:, :], T.raw[0:1, :], 128))

    v(V.tensor_copy(T.cdown[:, 0:1], T.cdi[:, rank:rank + 1]))
    v_zero = v(V.memset(T.v[:, :], 0.0))
    v(V.memset(T.xs[:, 4 * TOK:XW], 0.0))
    v(V.memset(T.m[:, :], BIG))
    A.wait_ge(sem.vv, v_zero)
    a_z = a_(A.activation(T.z[:, :], T.v[:, :], act.Copy))
    V.wait_ge(sem.gi, g_bc)
    for u in range(ND // 16):
        v(V.tensor_copy(T.tabl[:, 16 * u:16 * u + 16], T.bc[:, ND + u:2 * ND:ND // 16]))
        n = v(V.tensor_scalar(T.tabs[:, 16 * u:16 * u + 16], T.bc[:, u:ND:ND // 16], 4.0, None, op.mult))
    vneed(n)
    n = v(V.tensor_scalar(T.tabm[:, :], T.tabl[:, :], 4.0, None, op.mult))
    V.wait_ge(sem.dq, 16)
    v(V.quantize_mx(T.wq[:, :], T.wp[:, :], T.qwb[:, :]))
    vneed(n)
    vneed(v(V.tensor_tensor(T.tabe[:, :], T.tabs[:, :], T.tabm[:, :], op.add)))

    def end_of(s):
        return T.cs[:, CD * (s + 1):CD * (s + 1) + 1]

    def places_of(d):
        return end_of(S) if d == rank else T.cl[:, 2 * d:2 * d + 1]

    first = rank + rank % 2
    numbers = [T.cdl[:, first:first + 1], T.cdx[:, 0:S - 1], T.cdown[:, 0:1]]

    def part(s, lo, hi):
        return (T.h[:, 4 * CAP * s + 16 * lo:4 * CAP * s + 16 * hi],
                T.xs[:, :].indirect(T.off[:, OW * s + lo:OW * s + hi]))

    at, a_of = {}, {}

    def work(word):
        k = word[0]
        s = int(word[1:] or 0)
        c, w = slice(CAP * s, CAP * (s + 1)), slice(OW * s, OW * (s + 1))
        if k == "i":
            b = first + N
            x = v(V.tensor_copy(T.cdx[:, 0:S - 1], T.cdl[:, b:b + N * (S - 2) + 1:N]))
        elif k in "lgend":
            lo, hi = CD * LISTS[s][0], CD * LISTS[s][1]
            if k in "lge" and s == 1:
                vneed(at["i"])
            if k == "l":
                x = v(V.tensor_tensor(T.lm[:, lo:hi], T.tabl[:, :].indirect(numbers[s]), T.tri[:, lo:hi], op.mult))
            elif k == "g":
                x = v(V.tensor_copy(T.sg[:, lo:hi], T.tabs[:, :].indirect(numbers[s])))
            elif k == "e":
                x = v(V.tensor_copy(T.eg[:, lo + 1:hi + 1], T.tabe[:, :].indirect(numbers[s])))
            elif k == "n":
                vneed(at["l%d" % s])
                x = v(V.tensor_tensor_scan(T.cs[:, lo + 1:hi + 1], T.rst[:, lo:hi], T.lm[:, lo:hi], 0.0,
                                           op.mult, op.add))
            else:
                vneed(max(at["g%d" % s], at["e%d" % s]))
                x = v(V.tensor_tensor(T.dg[:, lo + 1:hi], T.sg[:, lo + 1:hi], T.eg[:, lo + 1:hi], op.subtract))
        elif k == "s":
            b = 0 if s == 0 else 2 if s == S else 1
            vneed(max(at["n%d" % b], at["d%d" % b]))
            x = v(V.tensor_copy(T.v[:, VW * s:VW * (s + 1)].indirect(end_of(s)), T.dg[:, CD * s + 1:CD * (s + 1) + 1]))
        elif k == "p":
            vneed(at["s%d" % s])
            x = v(V.tensor_tensor_scan(T.f[:, c], T.inc[:, :], T.v[:, VW * s:VW * s + CAP],
                                       T.sg[:, CD * s:CD * s + 1], op.add, op.add))
        elif k == "h":
            vneed(at["p%d" % s])
            x = v(V.tensor_tensor_scan(T.a[:, c], T.hold[:, :], T.f[:, c], 0.0, op.max, op.min))
        elif k == "c":
            vneed(at["h%d" % s])
            x = v(V.tensor_scalar(T.off[:, w], T.a[:, CAP * s + 3:CAP * (s + 1):4], T.pf[:, 3:4], None, op.subtract))
            A.wait_ge(sem.vv, x)
            o, i = part(s, 0, CUT[s])
            a_of[s] = a_(A.activation(o, i, act.Copy))
        elif k == "v":
            vneed(at["c%d" % s])
            o, i = part(s, CUT[s], OW)
            x = v(V.tensor_copy(o, i))
        elif k == "q":
            V.wait_ge(sem.aa, a_of[s])
            vneed(at.get("v%d" % s, 0))
            x = v(V.quantize_mx(T.q[:, c], T.p[:, c], T.h[:, 4 * CAP * s:4 * CAP * (s + 1)]))
        else:
            V.wait_ge(sem.cc, sum(share))
            for d in range(N):
                x = v(V.tensor_copy(T.m[:, VW * d:VW * (d + 1)].indirect(places_of(d)), T.neg[:, :]))
        at[word] = x

    for word in EARLY:
        work(word)
    A.wait_ge(sem.dx, 16)
    V.wait_ge(sem.dx, 16)
    V.wait_ge(sem.aa, a_z)
    V.wait_ge(sem.rq, rq_total)
    for word in ORDER:
        work(word)
    vneed(at["m"])

    def single(s, sm, o, i):
        a = topo.addr(T.cores[order[s]])
        g.remote_dma(o, i, remote_sem=sm, local_sem=sem.ls, pid=a[1], routing_id=a[0],
                     dma_engine_mask=topo.mask(core, T.cores[order[s]]))
        ln_[0] += len(eng[s])

    my_end = T.cl[:, 2 * rank:2 * rank + 1]
    g.wait_ge(sem.vv, max(at["n0"], at["n1"]))
    ts = []
    for s in range(4):
        es = eng[s][share[s] * s:share[s] * (s + 1)]
        ts.append(RemoteDMATransfer(dst_ids=[ids[s]], dma_engine_mask=bits(es), remote_sem=sem.cc,
                                    srcs=[end_of(s)], dsts=[my_end]))
        ln_[0] += len(es)
    g.remote_dma_fused(ts, local_sem=sem.ls)
    single(4, sem.cc, my_end, end_of(4))

    land = slice(CAP * rank, CAP * (rank + 1))
    for s in range(S):
        mine = slice(CAP * s, CAP * (s + 1))
        g.wait_ge(sem.vv, at["q%d" % s])
        single(s, sem["co%d" % rank], T.rc[:, land].bitcast(dt.uint8), T.q[:, mine].bitcast(dt.uint8))
        single(s, sem["pl%d" % rank], T.rp[:, land], T.p[:, mine])

    t_of = {}

    def product(b, cq, cp, k):
        E.matmul_mx(T.ps[:, 512 * b:512 * b + CAP], T.wq[:, :], T.wp[:, :], cq[:, k:k + CAP], cp[:, k:k + CAP],
                    True, True).then_inc(sem.tt, 1)
        tn[0] += 1
        t_of[b] = tn[0]
    turn = src[:OWN_AT] + [rank] + src[OWN_AT:]
    for d in turn:
        if d == rank:
            E.wait_ge(sem.vv, at["q%d" % S])
            product(rank, T.q, T.p, CAP * S)
        else:
            if not t_of:
                E.wait_ge(sem.vv, at["q0"])
            E.wait_ge(sem["co%d" % d], len(topo.engines(T.cores[d], core)))
            E.wait_ge(sem["pl%d" % d], len(topo.engines(T.cores[d], core)))
            product(d, T.rc, T.rp, CAP * d)

    for d in turn:
        V.wait_ge(sem.tt, t_of[d])
        n = v(V.tensor_tensor_scan(T.z[:, VW * d + 1:VW * d + CAP + 1], T.m[:, VW * d:VW * d + CAP],
                                   T.ps[:, 512 * d:512 * d + CAP], -BIG, op.min, op.max))
        o, i = T.ys[:, CD * d:CD * (d + 1)], T.z[:, VW * d:VW * (d + 1)].indirect(places_of(d))
        if d != turn[-1]:
            A.wait_ge(sem.vv, n)
            a_(A.activation(o, i, act.Copy))
        else:
            vneed(n)
            n = v(V.tensor_copy(o, i))
    Y.wait_ge(sem.aa, an[0])
    Y.wait_ge(sem.vv, n)
    Y.dma_start(T.y[:, :], T.ys[:, :]).then_inc(sem.dy, 16)
    Y.wait_ge(sem.dy, 16)
    g.wait_ge(sem.ls, ln_[0])
